import numpy as np
import ml_dtypes


def mxq(x, axis, fmt="e4m3"):
    dtype, down = {"e4m3": (ml_dtypes.float8_e4m3fn, 7), "e5m2": (ml_dtypes.float8_e5m2, 14)}[fmt]
    v = np.moveaxis(np.asarray(x, np.float32).astype(ml_dtypes.bfloat16).astype(np.float64), axis, -1)
    blocks = v.reshape(v.shape[:-1] + (-1, 32))
    amax = np.abs(blocks).max(-1, keepdims=True)
    byte = np.maximum(np.where(amax > 0, np.frexp(amax)[1] - 1 + 127, 0) - down, 1)
    scale = np.exp2(byte - 127.0)
    codes = (blocks / scale).astype(np.float32).astype(dtype).astype(np.float64)
    return np.moveaxis((codes * scale).reshape(v.shape), -1, axis)


WIDE = False


def mx_kscale(k):
    if not WIDE:
        return np.ones(k)
    levels = np.array([10, -10, 5, -5, 0])
    if k % 512:
        return np.exp2(np.random.permutation(np.resize(levels, k // 32))).repeat(32)
    a = np.empty((k // 512, 16))
    for p in range(k // 512):
        a[p, :8] = np.random.permutation(np.resize(levels, 8))
        for g in range(8):
            far = levels[np.abs(levels - a[p, g]) >= 10]
            a[p, g + 8] = far[np.random.randint(len(far))]
    return np.exp2(a.ravel()).repeat(32)


def f64(x):
    return np.asarray(x).astype(np.float64)


def striped(idx):
    return np.tile(idx.reshape(-1, 16).T, (8, 1)).astype(np.uint16)


def unstriped(offs):
    return offs[:16].T.reshape(-1).astype(np.int64)


def pack_weight(w):
    k, n = w.shape
    w = f64(np.asarray(w, np.float32).astype(ml_dtypes.bfloat16)).reshape(k // 32, 32, n)
    amax = np.abs(w).max(1)
    byte = np.clip(np.where(amax > 0, np.frexp(amax)[1] - 1 + 127 - 7, 1), 1, 254)
    scaled = (w * np.exp2(127.0 - byte)[:, None, :]).reshape(k, n).astype(np.float32)
    words = np.ascontiguousarray(scaled.reshape(k // 512, 128, 4, n).transpose(0, 1, 3, 2)).astype(ml_dtypes.float8_e4m3fn).view(np.uint8)
    return words, np.ascontiguousarray(byte.astype(np.uint8).reshape(k // 512, 16, n))


def unpack_weight(words, scales):
    g, p, n, _ = words.shape
    vals = np.ascontiguousarray(words).view(ml_dtypes.float8_e4m3fn).astype(np.float64) * np.repeat(np.exp2(scales.astype(np.float64) - 127.0), 8, axis=1)[..., None]
    return vals.transpose(0, 1, 3, 2).reshape(g * 512, n)


K, T, E, C, N = 1024, 1024, 16, 128, 128


def by_expert(wq, xq):
    return np.concatenate([wq[e].T @ xq[:, e * C:(e + 1) * C] for e in range(E)], axis=1)


def setup_inputs():
    n = np.random.standard_normal
    s = mx_kscale(K)[:, None]
    first = np.random.permutation(np.repeat(np.arange(E), T // E))
    second = (first + 1 + np.random.permutation(np.repeat(np.arange(E - 1), -(-T // (E - 1)))[:T])) % E
    while np.bincount(second, minlength=E).max() != T // E:
        load = np.bincount(second, minlength=E); hi, lo = int(load.argmax()), int(load.argmin())
        t = np.flatnonzero((second == hi) & (first != lo))[0]; second[t] = lo
    slot_token = np.empty(E * C, np.int64); pos = np.empty((2, T), np.int64); fill = np.zeros(E, np.int64)
    place = np.stack([np.random.permutation(C) for _ in range(E)])
    for r, deal in enumerate((first, second)):
        for t in np.random.permutation(T):
            e = deal[t]; j = e * C + place[e, fill[e]]; fill[e] += 1; slot_token[j] = t; pos[r, t] = j
    g = np.random.uniform(0.2, 0.8, T)
    packed = [pack_weight(m) for m in n((E, K, N)) / np.sqrt(K) / s[None]]
    return {
        "xT": (n((K, T)) * s).astype(np.float32),
        "w_words": np.stack([m[0] for m in packed]),
        "w_scales": np.stack([m[1] for m in packed]),
        "gate": np.stack([np.tile(g, (N, 1)), np.tile(1.0 - g, (N, 1))]).astype(np.float32),
        "offs": striped(slot_token),
        "pos1": striped(pos[0]),
        "pos2": striped(pos[1]),
    }


def reference(xT, w_words, w_scales, gate, offs, pos1, pos2):
    idx = unstriped(offs)
    xq = mxq(f64(xT)[:, idx], 0, "e4m3")
    w = np.stack([unpack_weight(w_words[e], w_scales[e]) for e in range(E)])
    y = by_expert(w, xq)
    return f64(gate[0]) * y[:, unstriped(pos1)] + f64(gate[1]) * y[:, unstriped(pos2)]

@@ -1,0 +1,138 @@
+from contextlib import ExitStack
+
+import concourse.mybir as mybir
+
+K, T, E, C, N = 1024, 1024, 16, 128, 128
+P = 128
+SLOTS = E * C
+PASSES = K // 512
+FLOPS = 2 * SLOTS * K * N
+
+F32 = mybir.dt.float32
+BF16 = mybir.dt.bfloat16
+I32 = mybir.dt.int32
+U32 = mybir.dt.uint32
+U16 = mybir.dt.uint16
+U8 = mybir.dt.uint8
+FP8X4 = mybir.dt.float8_e4m3fn_x4
+MULT = mybir.AluOpType.mult
+ADD = mybir.AluOpType.add
+
+X_CHUNKS = [
+    [(0, 512, 336), (512, 256, 176), (768, 256, 176)],
+    [(0, 512, 0), (512, 256, 0), (768, 256, 256)],
+]
+TOKEN_CHUNKS = [(0, 512), (512, 256), (768, 256)]
+BANKS = [(0, 4), (4, 4), (8, 4), (12, 2), (14, 1), (15, 1)]
+
+
+def tile_routed_moe_kernel(tc, xT, w_words, w_scales, gate, offs, pos1, pos2, out):
+    nc = tc.nc
+    with ExitStack() as ctx:
+        keep = ctx.enter_context(tc.tile_pool(name="keep", bufs=1))
+        psum = ctx.enter_context(tc.psum_pool(name="psum", bufs=1))
+
+        offs_t = keep.tile([P, SLOTS // 16], U16, name="offs_t")
+        pos1_t = keep.tile([P, T // 16], U16, name="pos1_t")
+        pos2_t = keep.tile([P, T // 16], U16, name="pos2_t")
+        w_t = keep.tile([P, E * PASSES, N], I32, name="w_t", align_bytes=64)
+        ws_t = keep.tile([P, E * PASSES, N], U8, name="ws_t", align_bytes=64)
+        words = [keep.tile([P, T], U32, name=f"words{a}", align_bytes=64) for a in range(PASSES)]
+        scales = keep.tile([P, T], U8, name="scales", align_bytes=64)
+        g_words = [keep.tile([P, SLOTS], U32, name=f"g_words{a}", align_bytes=64) for a in range(PASSES)]
+        g_scales = keep.tile([P, SLOTS], U8, name="g_scales", align_bytes=64)
+        gates = [keep.tile([P, T], F32, name=f"gate{r}") for r in range(2)]
+        y = keep.tile([P, SLOTS], F32, name="y")
+
+        nc.gpsimd.memset(scales[:], 0)
+        nc.vector.memset(ws_t[:].rearrange("p c n -> p (c n)").bitcast(I32), 0)
+
+        xv = xT.rearrange("(a p t) n -> a p t n", p=P, t=4)
+        raw = []
+        for a in range(PASSES):
+            raw.append([])
+            for c0, n, _ in X_CHUNKS[a]:
+                r = keep.tile([P, 4, n], F32, name=f"raw{a}_{c0}")
+                nc.sync.dma_start(out=r[:], in_=xv[a, :, :, c0 : c0 + n])
+                raw[a].append(r)
+            if a == 0:
+                nc.sync.dma_start(offs_t[:], offs)
+        for q in range(4):
+            nc.sync.dma_start(
+                out=ws_t[32 * q : 32 * q + 4, :, :].bitcast(I32),
+                in_=w_scales[:, :, 4 * q : 4 * q + 4, :].rearrange("e a r n -> r (e a) n").bitcast(I32),
+            )
+        for e in range(0, E, 4):
+            nc.sync.dma_start(
+                out=w_t[:, PASSES * e : PASSES * (e + 4), :],
+                in_=w_words[e : e + 4].rearrange("e a p n r -> p (e a) (n r)").bitcast(I32),
+            )
+        nc.sync.dma_start(pos1_t[:], pos1)
+        nc.sync.dma_start(pos2_t[:], pos2)
+        for r in range(2):
+            nc.sync.dma_start(out=gates[r][:], in_=gate[r])
+
+        def interleave(copy, grouped, r, j0, j1):
+            dst = grouped[:, 4 * j0 : 4 * j1].rearrange("p (c i t) -> p c t i", i=4, t=4)
+            src = r[:, :, j0:j1].rearrange("p t (c i) -> p c t i", i=4)
+            copy(dst, src)
+
+        def prepare(a):
+            for (c0, n, nv), r in zip_chunks(a):
+                grouped = keep.tile([P, 4 * n], BF16, name=f"grouped{a}_{c0}", align_bytes=64)
+                if nv > 0:
+                    interleave(nc.vector.tensor_copy, grouped, r, 0, nv)
+                if nv < n:
+                    interleave(nc.scalar.copy, grouped, r, nv, n)
+                nc.vector.quantize_mx(
+                    out=words[a][:, c0 : c0 + n].bitcast(FP8X4),
+                    scales=scales[4 * a : P, c0 : c0 + n],
+                    in_=grouped[:],
+                )
+
+        def zip_chunks(a):
+            return [(X_CHUNKS[a][i], raw[a][i]) for i in range(len(raw[a]))]
+
+        def fetch(dst, window, s0, s1):
+            nc.vector.tensor_copy(dst[:, s0:s1], window[:].indirect(offs_t[:, s0 // 16 : s1 // 16]))
+
+        def expert(e, bank, j):
+            for a in range(PASSES):
+                c = PASSES * e + a
+                cols = slice(e * C, (e + 1) * C)
+                nc.tensor.matmul_mx(
+                    out=bank[:, j * C : (j + 1) * C],
+                    lhsT=w_t[:, c, :].bitcast(FP8X4),
+                    lhsT_scale=ws_t[:, c, :],
+                    rhs=g_words[a][:, cols].bitcast(FP8X4),
+                    rhs_scale=g_scales[4 * a : P, cols],
+                    start=(a == 0),
+                    stop=(a == PASSES - 1),
+                )
+
+        prepare(0)
+        for s0, s1 in ((0, 768), (768, 1536), (1536, 2048)):
+            fetch(g_words[0], words[0], s0, s1)
+        prepare(1)
+        for s0, s1 in ((0, 768), (768, 1536), (1536, 2048)):
+            fetch(g_scales, scales, s0, s1)
+        for s0, s1 in ((0, 768), (768, 1536), (1536, 1792), (1792, 2048)):
+            fetch(g_words[1], words[1], s0, s1)
+        for b, (e0, count) in enumerate(BANKS):
+            bank = psum.tile([P, 512], F32, name=f"bank{b}")
+            for j in range(count):
+                expert(e0 + j, bank, j)
+            copy = nc.vector.tensor_copy if e0 == E - 1 else nc.scalar.copy
+            copy(y[:, e0 * C : (e0 + count) * C], bank[:, 0 : count * C])
+
+        first = keep.tile([P, T], F32, name="first")
+        second = keep.tile([P, T], F32, name="second")
+        nc.vector.tensor_tensor(first[:], y[:].indirect(pos1_t[:]), gates[0][:], MULT)
+        for t0, n in TOKEN_CHUNKS:
+            cols = slice(t0, t0 + n)
+            nc.vector.tensor_tensor(
+                second[:, cols], y[:].indirect(pos2_t[:, t0 // 16 : (t0 + n) // 16]), gates[1][:, cols], MULT
+            )
+            res = keep.tile([P, n], F32, name=f"res{t0}")
+            nc.vector.tensor_tensor(res[:], first[:, cols], second[:, cols], ADD)
+            nc.sync.dma_start(out=out[:, cols], in_=res[:])

@@ -20,9 +20,13 @@ ADD = mybir.AluOpType.add
 
 X_CHUNKS = [
     [(0, 512, 336), (512, 256, 176), (768, 256, 176)],
-    [(0, 512, 0), (512, 256, 0), (768, 256, 256)],
+    [(0, 256, 0), (256, 256, 0), (512, 256, 0), (768, 256, 0)],
 ]
-TOKEN_CHUNKS = [(0, 512), (512, 256), (768, 256)]
+QUANT_CHUNKS = [
+    [(0, 512), (512, 256), (768, 256)],
+    [(0, 512), (512, 512)],
+]
+TOKEN_CHUNKS = [(0, 512), (512, 384), (896, 128)]
 BANKS = [(0, 4), (4, 4), (8, 4), (12, 2), (14, 1), (15, 1)]
 
 
@@ -77,21 +81,28 @@ def tile_routed_moe_kernel(tc, xT, w_words, w_scales, gate, offs, pos1, pos2, ou
             src = r[:, :, j0:j1].rearrange("p t (c i) -> p c t i", i=4)
             copy(dst, src)
 
-        def prepare(a):
-            for (c0, n, nv), r in zip_chunks(a):
-                grouped = keep.tile([P, 4 * n], BF16, name=f"grouped{a}_{c0}", align_bytes=64)
-                if nv > 0:
-                    interleave(nc.vector.tensor_copy, grouped, r, 0, nv)
-                if nv < n:
-                    interleave(nc.scalar.copy, grouped, r, nv, n)
-                nc.vector.quantize_mx(
-                    out=words[a][:, c0 : c0 + n].bitcast(FP8X4),
-                    scales=scales[4 * a : P, c0 : c0 + n],
-                    in_=grouped[:],
-                )
+        grouped = [
+            [keep.tile([P, 4 * qn], BF16, name=f"grouped{a}_{q0}", align_bytes=64) for q0, qn in QUANT_CHUNKS[a]]
+            for a in range(PASSES)
+        ]
 
-        def zip_chunks(a):
-            return [(X_CHUNKS[a][i], raw[a][i]) for i in range(len(raw[a]))]
+        def arrange(a, i):
+            c0, n, nv = X_CHUNKS[a][i]
+            for (q0, qn), tile in zip(QUANT_CHUNKS[a], grouped[a]):
+                if q0 <= c0 < q0 + qn:
+                    part = tile[:, 4 * (c0 - q0) : 4 * (c0 - q0 + n)]
+                    if nv > 0:
+                        interleave(nc.vector.tensor_copy, part, raw[a][i], 0, nv)
+                    if nv < n:
+                        interleave(nc.scalar.copy, part, raw[a][i], nv, n)
+
+        def quantise(a, i):
+            q0, qn = QUANT_CHUNKS[a][i]
+            nc.vector.quantize_mx(
+                out=words[a][:, q0 : q0 + qn].bitcast(FP8X4),
+                scales=scales[4 * a : P, q0 : q0 + qn],
+                in_=grouped[a][i][:],
+            )
 
         def fetch(dst, window, s0, s1):
             nc.vector.tensor_copy(dst[:, s0:s1], window[:].indirect(offs_t[:, s0 // 16 : s1 // 16]))
@@ -110,10 +121,19 @@ def tile_routed_moe_kernel(tc, xT, w_words, w_scales, gate, offs, pos1, pos2, ou
                     stop=(a == PASSES - 1),
                 )
 
-        prepare(0)
-        for s0, s1 in ((0, 768), (768, 1536), (1536, 2048)):
-            fetch(g_words[0], words[0], s0, s1)
-        prepare(1)
+        arrange(0, 0)
+        arrange(0, 1)
+        quantise(0, 0)
+        arrange(0, 2)
+        quantise(0, 1)
+        quantise(0, 2)
+        for i in range(4):
+            arrange(1, i)
+        fetch(g_words[0], words[0], 0, 768)
+        fetch(g_words[0], words[0], 768, 1536)
+        quantise(1, 0)
+        fetch(g_words[0], words[0], 1536, 2048)
+        quantise(1, 1)
         for s0, s1 in ((0, 768), (768, 1536), (1536, 2048)):
             fetch(g_scales, scales, s0, s1)
         for s0, s1 in ((0, 768), (768, 1536), (1536, 1792), (1792, 2048)):
@@ -128,11 +148,20 @@ def tile_routed_moe_kernel(tc, xT, w_words, w_scales, gate, offs, pos1, pos2, ou
         first = keep.tile([P, T], F32, name="first")
         second = keep.tile([P, T], F32, name="second")
         nc.vector.tensor_tensor(first[:], y[:].indirect(pos1_t[:]), gates[0][:], MULT)
-        for t0, n in TOKEN_CHUNKS:
+        def fetch_second(t0, n):
             cols = slice(t0, t0 + n)
             nc.vector.tensor_tensor(
                 second[:, cols], y[:].indirect(pos2_t[:, t0 // 16 : (t0 + n) // 16]), gates[1][:, cols], MULT
             )
+
+        def finish(t0, n):
+            cols = slice(t0, t0 + n)
             res = keep.tile([P, n], F32, name=f"res{t0}")
             nc.vector.tensor_tensor(res[:], first[:, cols], second[:, cols], ADD)
             nc.sync.dma_start(out=out[:, cols], in_=res[:])
+
+        fetch_second(*TOKEN_CHUNKS[0])
+        for i in range(1, len(TOKEN_CHUNKS)):
+            fetch_second(*TOKEN_CHUNKS[i])
+            finish(*TOKEN_CHUNKS[i - 1])
+        finish(*TOKEN_CHUNKS[-1])

@@ -6,6 +6,7 @@ K, T, E, C, N = 1024, 1024, 16, 128, 128
 P = 128
 SLOTS = E * C
 PASSES = K // 512
+WINDOW = 2 * T
 FLOPS = 2 * SLOTS * K * N
 
 F32 = mybir.dt.float32
@@ -19,11 +20,11 @@ MULT = mybir.AluOpType.mult
 ADD = mybir.AluOpType.add
 
 X_CHUNKS = [
-    [(0, 512, 336), (512, 256, 176), (768, 256, 176)],
-    [(0, 256, 0), (256, 256, 0), (512, 256, 0), (768, 256, 0)],
+    [(0, 640, 400), (640, 256, 144), (896, 128, 64)],
+    [(0, 256, 0), (256, 256, 0), (512, 256, 0), (768, 128, 0), (896, 128, 0)],
 ]
 QUANT_CHUNKS = [
-    [(0, 512), (512, 256), (768, 256)],
+    [(0, 512), (512, 128), (640, 256), (896, 128)],
     [(0, 512), (512, 512)],
 ]
 TOKEN_CHUNKS = [(0, 512), (512, 384), (896, 128)]
@@ -41,14 +42,14 @@ def tile_routed_moe_kernel(tc, xT, w_words, w_scales, gate, offs, pos1, pos2, ou
         pos2_t = keep.tile([P, T // 16], U16, name="pos2_t")
         w_t = keep.tile([P, E * PASSES, N], I32, name="w_t", align_bytes=64)
         ws_t = keep.tile([P, E * PASSES, N], U8, name="ws_t", align_bytes=64)
-        words = [keep.tile([P, T], U32, name=f"words{a}", align_bytes=64) for a in range(PASSES)]
-        scales = keep.tile([P, T], U8, name="scales", align_bytes=64)
+        words = [keep.tile([P, WINDOW], U32, name=f"words{a}", align_bytes=64) for a in range(PASSES)]
+        scales = keep.tile([P, WINDOW], U8, name="scales", align_bytes=64)
         g_words = [keep.tile([P, SLOTS], U32, name=f"g_words{a}", align_bytes=64) for a in range(PASSES)]
         g_scales = keep.tile([P, SLOTS], U8, name="g_scales", align_bytes=64)
         gates = [keep.tile([P, T], F32, name=f"gate{r}") for r in range(2)]
         y = keep.tile([P, SLOTS], F32, name="y")
 
-        nc.gpsimd.memset(scales[:], 0)
+        nc.gpsimd.memset(scales[:, 0:T], 0)
         nc.vector.memset(ws_t[:].rearrange("p c n -> p (c n)").bitcast(I32), 0)
 
         xv = xT.rearrange("(a p t) n -> a p t n", p=P, t=4)
@@ -81,27 +82,22 @@ def tile_routed_moe_kernel(tc, xT, w_words, w_scales, gate, offs, pos1, pos2, ou
             src = r[:, :, j0:j1].rearrange("p t (c i) -> p c t i", i=4)
             copy(dst, src)
 
-        grouped = [
-            [keep.tile([P, 4 * qn], BF16, name=f"grouped{a}_{q0}", align_bytes=64) for q0, qn in QUANT_CHUNKS[a]]
-            for a in range(PASSES)
-        ]
+        grouped = [keep.tile([P, 4 * T], BF16, name=f"grouped{a}", align_bytes=64) for a in range(PASSES)]
 
         def arrange(a, i):
             c0, n, nv = X_CHUNKS[a][i]
-            for (q0, qn), tile in zip(QUANT_CHUNKS[a], grouped[a]):
-                if q0 <= c0 < q0 + qn:
-                    part = tile[:, 4 * (c0 - q0) : 4 * (c0 - q0 + n)]
-                    if nv > 0:
-                        interleave(nc.vector.tensor_copy, part, raw[a][i], 0, nv)
-                    if nv < n:
-                        interleave(nc.scalar.copy, part, raw[a][i], nv, n)
+            part = grouped[a][:, 4 * c0 : 4 * (c0 + n)]
+            if nv > 0:
+                interleave(nc.vector.tensor_copy, part, raw[a][i], 0, nv)
+            if nv < n:
+                interleave(nc.scalar.copy, part, raw[a][i], nv, n)
 
         def quantise(a, i):
             q0, qn = QUANT_CHUNKS[a][i]
             nc.vector.quantize_mx(
                 out=words[a][:, q0 : q0 + qn].bitcast(FP8X4),
                 scales=scales[4 * a : P, q0 : q0 + qn],
-                in_=grouped[a][i][:],
+                in_=grouped[a][:, 4 * q0 : 4 * (q0 + qn)],
             )
 
         def fetch(dst, window, s0, s1):
@@ -124,26 +120,27 @@ def tile_routed_moe_kernel(tc, xT, w_words, w_scales, gate, offs, pos1, pos2, ou
         arrange(0, 0)
         arrange(0, 1)
         quantise(0, 0)
-        arrange(0, 2)
         quantise(0, 1)
+        arrange(0, 2)
         quantise(0, 2)
-        for i in range(4):
+        quantise(0, 3)
+        for i in range(len(X_CHUNKS[1])):
             arrange(1, i)
-        fetch(g_words[0], words[0], 0, 768)
-        fetch(g_words[0], words[0], 768, 1536)
+        fetch(g_words[0], words[0], 0, 1536)
         quantise(1, 0)
         fetch(g_words[0], words[0], 1536, 2048)
         quantise(1, 1)
-        for s0, s1 in ((0, 768), (768, 1536), (1536, 2048)):
-            fetch(g_scales, scales, s0, s1)
-        for s0, s1 in ((0, 768), (768, 1536), (1536, 1792), (1792, 2048)):
-            fetch(g_words[1], words[1], s0, s1)
+        fetch(g_words[1], words[1], 0, 1536)
+        fetch(g_scales, scales, 0, 512)
+        fetch(g_scales, scales, 512, 1536)
+        fetch(g_words[1], words[1], 1536, 2048)
+        fetch(g_scales, scales, 1536, 1792)
+        fetch(g_scales, scales, 1792, 2048)
         for b, (e0, count) in enumerate(BANKS):
             bank = psum.tile([P, 512], F32, name=f"bank{b}")
             for j in range(count):
                 expert(e0 + j, bank, j)
-            copy = nc.vector.tensor_copy if e0 == E - 1 else nc.scalar.copy
-            copy(y[:, e0 * C : (e0 + count) * C], bank[:, 0 : count * C])
+            nc.scalar.copy(y[:, e0 * C : (e0 + count) * C], bank[:, 0 : count * C])
 
         first = keep.tile([P, T], F32, name="first")
         second = keep.tile([P, T], F32, name="second")

@@ -25,10 +25,10 @@ X_CHUNKS = [
 ]
 QUANT_CHUNKS = [
     [(0, 512), (512, 128), (640, 256), (896, 128)],
-    [(0, 512), (512, 512)],
+    [(0, 512), (512, 256), (768, 256)],
 ]
 TOKEN_CHUNKS = [(0, 512), (512, 384), (896, 128)]
-BANKS = [(0, 4), (4, 4), (8, 4), (12, 2), (14, 1), (15, 1)]
+BANKS = [(0, 3), (3, 3), (6, 3), (9, 3), (12, 2), (14, 1), (15, 1)]
 
 
 def tile_routed_moe_kernel(tc, xT, w_words, w_scales, gate, offs, pos1, pos2, out):
@@ -130,9 +130,10 @@ def tile_routed_moe_kernel(tc, xT, w_words, w_scales, gate, offs, pos1, pos2, ou
         quantise(1, 0)
         fetch(g_words[0], words[0], 1536, 2048)
         quantise(1, 1)
+        quantise(1, 2)
         fetch(g_words[1], words[1], 0, 1536)
-        fetch(g_scales, scales, 0, 512)
-        fetch(g_scales, scales, 512, 1536)
+        fetch(g_scales, scales, 0, 768)
+        fetch(g_scales, scales, 768, 1536)
         fetch(g_words[1], words[1], 1536, 2048)
         fetch(g_scales, scales, 1536, 1792)
         fetch(g_scales, scales, 1792, 2048)

from contextlib import ExitStack

import concourse.mybir as mybir

K, T, E, C, N = 1024, 1024, 16, 128, 128
P = 128
SLOTS = E * C
PASSES = K // 512
WINDOW = 2 * T
FLOPS = 2 * SLOTS * K * N

F32 = mybir.dt.float32
BF16 = mybir.dt.bfloat16
I32 = mybir.dt.int32
U32 = mybir.dt.uint32
U16 = mybir.dt.uint16
U8 = mybir.dt.uint8
FP8X4 = mybir.dt.float8_e4m3fn_x4
MULT = mybir.AluOpType.mult
ADD = mybir.AluOpType.add

X_CHUNKS = [
    [(0, 640, 400), (640, 256, 144), (896, 128, 64)],
    [(0, 256, 0), (256, 256, 0), (512, 256, 0), (768, 128, 0), (896, 128, 0)],
]
QUANT_CHUNKS = [
    [(0, 512), (512, 128), (640, 256), (896, 128)],
    [(0, 512), (512, 256), (768, 256)],
]
TOKEN_CHUNKS = [(0, 512), (512, 384), (896, 128)]
BANKS = [(0, 3), (3, 3), (6, 3), (9, 3), (12, 2), (14, 1), (15, 1)]


def tile_routed_moe_kernel(tc, xT, w_words, w_scales, gate, offs, pos1, pos2, out):
    nc = tc.nc
    with ExitStack() as ctx:
        keep = ctx.enter_context(tc.tile_pool(name="keep", bufs=1))
        psum = ctx.enter_context(tc.psum_pool(name="psum", bufs=1))

        offs_t = keep.tile([P, SLOTS // 16], U16, name="offs_t")
        pos1_t = keep.tile([P, T // 16], U16, name="pos1_t")
        pos2_t = keep.tile([P, T // 16], U16, name="pos2_t")
        w_t = keep.tile([P, E * PASSES, N], I32, name="w_t", align_bytes=64)
        ws_t = keep.tile([P, E * PASSES, N], U8, name="ws_t", align_bytes=64)
        words = [keep.tile([P, WINDOW], U32, name=f"words{a}", align_bytes=64) for a in range(PASSES)]
        scales = keep.tile([P, WINDOW], U8, name="scales", align_bytes=64)
        g_words = [keep.tile([P, SLOTS], U32, name=f"g_words{a}", align_bytes=64) for a in range(PASSES)]
        g_scales = keep.tile([P, SLOTS], U8, name="g_scales", align_bytes=64)
        gates = [keep.tile([P, T], F32, name=f"gate{r}") for r in range(2)]
        y = keep.tile([P, SLOTS], F32, name="y")

        nc.gpsimd.memset(scales[:, 0:T], 0)
        nc.vector.memset(ws_t[:].rearrange("p c n -> p (c n)").bitcast(I32), 0)

        xv = xT.rearrange("(a p t) n -> a p t n", p=P, t=4)
        raw = []
        for a in range(PASSES):
            raw.append([])
            for c0, n, _ in X_CHUNKS[a]:
                r = keep.tile([P, 4, n], F32, name=f"raw{a}_{c0}")
                nc.sync.dma_start(out=r[:], in_=xv[a, :, :, c0 : c0 + n])
                raw[a].append(r)
            if a == 0:
                nc.sync.dma_start(offs_t[:], offs)
        for q in range(4):
            nc.sync.dma_start(
                out=ws_t[32 * q : 32 * q + 4, :, :].bitcast(I32),
                in_=w_scales[:, :, 4 * q : 4 * q + 4, :].rearrange("e a r n -> r (e a) n").bitcast(I32),
            )
        for e in range(0, E, 4):
            nc.sync.dma_start(
                out=w_t[:, PASSES * e : PASSES * (e + 4), :],
                in_=w_words[e : e + 4].rearrange("e a p n r -> p (e a) (n r)").bitcast(I32),
            )
        nc.sync.dma_start(pos1_t[:], pos1)
        nc.sync.dma_start(pos2_t[:], pos2)
        for r in range(2):
            nc.sync.dma_start(out=gates[r][:], in_=gate[r])

        def interleave(copy, grouped, r, j0, j1):
            dst = grouped[:, 4 * j0 : 4 * j1].rearrange("p (c i t) -> p c t i", i=4, t=4)
            src = r[:, :, j0:j1].rearrange("p t (c i) -> p c t i", i=4)
            copy(dst, src)

        grouped = [keep.tile([P, 4 * T], BF16, name=f"grouped{a}", align_bytes=64) for a in range(PASSES)]

        def arrange(a, i):
            c0, n, nv = X_CHUNKS[a][i]
            part = grouped[a][:, 4 * c0 : 4 * (c0 + n)]
            if nv > 0:
                interleave(nc.vector.tensor_copy, part, raw[a][i], 0, nv)
            if nv < n:
                interleave(nc.scalar.copy, part, raw[a][i], nv, n)

        def quantise(a, i):
            q0, qn = QUANT_CHUNKS[a][i]
            nc.vector.quantize_mx(
                out=words[a][:, q0 : q0 + qn].bitcast(FP8X4),
                scales=scales[4 * a : P, q0 : q0 + qn],
                in_=grouped[a][:, 4 * q0 : 4 * (q0 + qn)],
            )

        def fetch(dst, window, s0, s1):
            nc.vector.tensor_copy(dst[:, s0:s1], window[:].indirect(offs_t[:, s0 // 16 : s1 // 16]))

        def expert(e, bank, j):
            for a in range(PASSES):
                c = PASSES * e + a
                cols = slice(e * C, (e + 1) * C)
                nc.tensor.matmul_mx(
                    out=bank[:, j * C : (j + 1) * C],
                    lhsT=w_t[:, c, :].bitcast(FP8X4),
                    lhsT_scale=ws_t[:, c, :],
                    rhs=g_words[a][:, cols].bitcast(FP8X4),
                    rhs_scale=g_scales[4 * a : P, cols],
                    start=(a == 0),
                    stop=(a == PASSES - 1),
                )

        arrange(0, 0)
        arrange(0, 1)
        quantise(0, 0)
        quantise(0, 1)
        arrange(0, 2)
        quantise(0, 2)
        quantise(0, 3)
        for i in range(len(X_CHUNKS[1])):
            arrange(1, i)
        fetch(g_words[0], words[0], 0, 1536)
        quantise(1, 0)
        fetch(g_words[0], words[0], 1536, 2048)
        quantise(1, 1)
        quantise(1, 2)
        fetch(g_words[1], words[1], 0, 1536)
        fetch(g_scales, scales, 0, 768)
        fetch(g_scales, scales, 768, 1536)
        fetch(g_words[1], words[1], 1536, 2048)
        fetch(g_scales, scales, 1536, 1792)
        fetch(g_scales, scales, 1792, 2048)
        for b, (e0, count) in enumerate(BANKS):
            bank = psum.tile([P, 512], F32, name=f"bank{b}")
            for j in range(count):
                expert(e0 + j, bank, j)
            nc.scalar.copy(y[:, e0 * C : (e0 + count) * C], bank[:, 0 : count * C])

        first = keep.tile([P, T], F32, name="first")
        second = keep.tile([P, T], F32, name="second")
        nc.vector.tensor_tensor(first[:], y[:].indirect(pos1_t[:]), gates[0][:], MULT)
        def fetch_second(t0, n):
            cols = slice(t0, t0 + n)
            nc.vector.tensor_tensor(
                second[:, cols], y[:].indirect(pos2_t[:, t0 // 16 : (t0 + n) // 16]), gates[1][:, cols], MULT
            )

        def finish(t0, n):
            cols = slice(t0, t0 + n)
            res = keep.tile([P, n], F32, name=f"res{t0}")
            nc.vector.tensor_tensor(res[:], first[:, cols], second[:, cols], ADD)
            nc.sync.dma_start(out=out[:, cols], in_=res[:])

        fetch_second(*TOKEN_CHUNKS[0])
        for i in range(1, len(TOKEN_CHUNKS)):
            fetch_second(*TOKEN_CHUNKS[i])
            finish(*TOKEN_CHUNKS[i - 1])
        finish(*TOKEN_CHUNKS[-1])
